import numpy as np
import ml_dtypes


def mxq(x, axis, fmt="e4m3"):
    dtype, down = {"e4m3": (ml_dtypes.float8_e4m3fn, 7), "e5m2": (ml_dtypes.float8_e5m2, 14)}[fmt]
    v = np.moveaxis(np.asarray(x, np.float32).astype(ml_dtypes.bfloat16).astype(np.float64), axis, -1)
    blocks = v.reshape(v.shape[:-1] + (-1, 32))
    amax = np.abs(blocks).max(-1, keepdims=True)
    byte = np.maximum(np.where(amax > 0, np.frexp(amax)[1] - 1 + 127, 0) - down, 1)
    scale = np.exp2(byte - 127.0)
    codes = (blocks / scale).astype(np.float32).astype(dtype).astype(np.float64)
    return np.moveaxis((codes * scale).reshape(v.shape), -1, axis)


WIDE = False


def mx_kscale(k):
    if not WIDE:
        return np.ones(k)
    levels = np.array([10, -10, 5, -5, 0])
    if k % 512:
        return np.exp2(np.random.permutation(np.resize(levels, k // 32))).repeat(32)
    a = np.empty((k // 512, 16))
    for p in range(k // 512):
        a[p, :8] = np.random.permutation(np.resize(levels, 8))
        for g in range(8):
            far = levels[np.abs(levels - a[p, g]) >= 10]
            a[p, g + 8] = far[np.random.randint(len(far))]
    return np.exp2(a.ravel()).repeat(32)


def f64(x):
    return np.asarray(x).astype(np.float64)


def striped(idx):
    return np.tile(idx.reshape(-1, 16).T, (8, 1)).astype(np.uint16)


def unstriped(offs):
    return offs[:16].T.reshape(-1).astype(np.int64)


def pack_weight(w):
    k, n = w.shape
    w = f64(np.asarray(w, np.float32).astype(ml_dtypes.bfloat16)).reshape(k // 32, 32, n)
    amax = np.abs(w).max(1)
    byte = np.clip(np.where(amax > 0, np.frexp(amax)[1] - 1 + 127 - 7, 1), 1, 254)
    scaled = (w * np.exp2(127.0 - byte)[:, None, :]).reshape(k, n).astype(np.float32)
    words = np.ascontiguousarray(scaled.reshape(k // 512, 128, 4, n).transpose(0, 1, 3, 2)).astype(ml_dtypes.float8_e4m3fn).view(np.uint8)
    return words, np.ascontiguousarray(byte.astype(np.uint8).reshape(k // 512, 16, n))


def unpack_weight(words, scales):
    g, p, n, _ = words.shape
    vals = np.ascontiguousarray(words).view(ml_dtypes.float8_e4m3fn).astype(np.float64) * np.repeat(np.exp2(scales.astype(np.float64) - 127.0), 8, axis=1)[..., None]
    return vals.transpose(0, 1, 3, 2).reshape(g * 512, n)


def relu(v):
    return np.maximum(v, 0.0)


def sigmoid(v):
    return 1.0 / (1.0 + np.exp(-np.maximum(v, -700.0)))


K, T, S, D, N = 512, 2048, 512, 4, 256
P = 2 ** 7


def setup_inputs():
    n = np.random.standard_normal
    s = mx_kscale(K)[:, None]
    packed_xT = pack_weight(n((K, T)) * s)
    return {
        "x_words": packed_xT[0],
        "x_scales": packed_xT[1],
        "w1": (n((K, N)) / np.sqrt(K) / s).astype(np.float32),
        "w2": (n((K, N)) / np.sqrt(K) / s).astype(np.float32),
        "w3": (n((K, N)) / np.sqrt(K) / s).astype(np.float32),
        "fmax": (np.tile(np.random.uniform(0.6, 1.8, S), (P, 1))).astype(np.float32),
        "wl": (np.random.uniform(0.2, 0.8, (N, 1))).astype(np.float32),
        "offs": striped(np.random.permutation(T)[:S]),
    }


def reference(x_words, x_scales, w1, w2, w3, fmax, wl, offs):
    xq = unpack_weight(x_words, x_scales)[:, unstriped(offs)]
    ya = mxq(f64(w3), 0, "e4m3").T @ xq
    actv = sigmoid(ya)
    yl = mxq(f64(w1), 0, "e4m3").T @ xq
    flen = np.exp(-0.8 * ((yl) ** 2))
    yv = mxq(f64(w2), 0, "e4m3").T @ xq
    vel = np.tanh(yv)
    fvel = (-1.0 * vel + 1.0) / (0.6 * vel + 1.3)
    frc = f64(fmax)[:1] * ((actv * flen) * fvel + 0.4 * (relu(np.exp(0.9 * yl) - 1.0)))
    pw = frc * np.abs(vel) + 0.3 * ((actv) ** 2)
    return pw.reshape(len(pw), -1, D).sum(axis=2) - (f64(wl) * (frc.reshape(len(frc), -1, D).max(axis=2)))

@@ -1,0 +1,137 @@
+import math
+from contextlib import ExitStack
+
+import concourse.mybir as mybir
+
+K, T, S, D, N = 512, 2048, 512, 4, 256
+P = 128
+PACK = 4
+V = S // D
+HALVES = N // P
+FLOPS = 3 * 2 * K * N * S
+
+F32 = mybir.dt.float32
+BF16 = mybir.dt.bfloat16
+I32 = mybir.dt.int32
+U32 = mybir.dt.uint32
+U16 = mybir.dt.uint16
+U8 = mybir.dt.uint8
+FP8X4 = mybir.dt.float8_e4m3fn_x4
+ALU = mybir.AluOpType
+ACT = mybir.ActivationFunctionType
+
+VEL_SHIFT = 0.5 * math.log(1.9 / 0.7)
+SQ_WEIGHT = 0.3 / 4
+
+
+def tile_picked_yhillm_eff_p_kernel(tc, x_words, x_scales, w1, w2, w3, fmax, wl, offs, out):
+    nc = tc.nc
+    with ExitStack() as ctx:
+        keep = ctx.enter_context(tc.tile_pool(name="keep", bufs=1))
+        work = ctx.enter_context(tc.tile_pool(name="work", bufs=2))
+        psum = ctx.enter_context(tc.psum_pool(name="psum", bufs=1))
+
+        offsets = keep.tile([P, S // 16], U16, name="offsets")
+        nc.sync.dma_start(offsets[:], offs)
+
+        scale_table = keep.tile([P, T], U8, name="scale_table", align_bytes=64)
+        nc.vector.memset(scale_table[:].bitcast(I32), 0)
+        for q in range(4):
+            nc.scalar.dma_start(
+                scale_table[32 * q : 32 * q + 4, :].bitcast(I32),
+                x_scales[0, 4 * q : 4 * q + 4, :].bitcast(I32),
+            )
+        word_table = keep.tile([P, T], I32, name="word_table", align_bytes=64)
+        nc.sync.dma_start(word_table[:], x_words[0].rearrange("p c r -> p (c r)").bitcast(I32))
+
+        zeros = keep.tile([P, P], F32, name="zeros", tag="floats")
+        nc.vector.memset(zeros[:], 0.0)
+        ident = keep.tile([P, P], F32, name="ident")
+        nc.gpsimd.affine_select(out=ident[:], in_=zeros[:], compare_op=ALU.not_equal, fill=1.0, base=0,
+                                pattern=[[-1, P]], channel_multiplier=1)
+
+        floats = keep.tile([P, 3 * PACK * N + 16], F32, name="floats", tag="floats")
+        raw = {}
+        for i, (name, w) in enumerate((("len", w1), ("act", w3), ("vel", w2))):
+            raw[name] = floats[:, i * PACK * N : (i + 1) * PACK * N].rearrange("p (j c) -> p j c", j=PACK)
+            nc.sync.dma_start(raw[name], w.rearrange("(p j) c -> p j c", j=PACK))
+        force = floats[:, 3 * PACK * N : 3 * PACK * N + D]
+        nc.sync.dma_start(force, fmax[0, :].rearrange("(v d) -> v d", d=D))
+        peak_w = floats[:, 3 * PACK * N + 8 : 3 * PACK * N + 8 + HALVES]
+        with nc.allow_non_contiguous_dma(reason="one weight a task row"):
+            nc.sync.dma_start(peak_w, wl.rearrange("(h p) o -> p (h o)", p=P))
+
+        picked_scales = keep.tile([P, S], U8, name="picked_scales", align_bytes=64)
+        nc.vector.tensor_copy(picked_scales[:], scale_table[:].indirect(offsets[:]))
+        x_scale = keep.tile([P, D, V], U8, name="x_scale", align_bytes=64)
+        nc.vector.tensor_copy(x_scale[:], picked_scales[:].rearrange("p (v d) -> p d v", d=D))
+        x_codes = keep.tile([P, D, V], U32, name="x_codes", align_bytes=64)
+        nc.vector.tensor_copy(x_codes[:].rearrange("p d v -> p v d"), word_table[:].bitcast(U32).indirect(offsets[:]))
+
+        def weave(name, h, on_scalar):
+            grouped = keep.tile([P, P, PACK], BF16, name="grouped_%s%d" % (name, h), align_bytes=64)
+            dst = grouped[:].rearrange("p (c i) j -> p c j i", i=4)
+            src = raw[name][:, :, h * P : (h + 1) * P].rearrange("p j (c i) -> p c j i", i=4)
+            if on_scalar:
+                nc.scalar.activation(dst, src, ACT.Copy)
+            else:
+                nc.vector.tensor_copy(dst, src)
+            return grouped
+
+        def product(name, h, grouped):
+            codes = keep.tile([P, P], U32, name="codes_%s%d" % (name, h), align_bytes=64)
+            scales = keep.tile([P, P], U8, name="scales_%s%d" % (name, h), align_bytes=64)
+            nc.vector.quantize_mx(out=codes[:].bitcast(FP8X4), scales=scales[:], in_=grouped[:].rearrange("p c j -> p (c j)"))
+            y = psum.tile([P, D, P], F32, name="y_%s%d" % (name, h))
+            for d in range(D):
+                nc.tensor.matmul_mx(
+                    out=y[:, d, :], lhsT=x_codes[:, d, :].bitcast(FP8X4), lhsT_scale=x_scale[:, d, :],
+                    rhs=codes[:].bitcast(FP8X4), rhs_scale=scales[:], start=True, stop=True,
+                )
+            return y
+
+        y = {}
+        for name in ("len", "act", "vel"):
+            g = [weave(name, h, name == "len") for h in range(HALVES)]
+            for h in range(HALVES):
+                y[name, h] = product(name, h, g[h])
+
+        def buf(name):
+            return work.tile([P, D, P], F32, name=name)
+
+        for h in range(HALVES):
+            yl, ya, yv = y["len", h], y["act", h], y["vel", h]
+            sq, bell, grow, ta, tb, vel, speed = [buf(n) for n in ("sq", "bell", "grow", "ta", "tb", "vel", "speed")]
+            nc.scalar.activation(sq[:], yl[:], ACT.Square)
+            nc.scalar.activation(grow[:], yl[:], ACT.Exp, scale=0.9, bias=math.log(0.4))
+            nc.scalar.activation(bell[:], sq[:], ACT.Exp, scale=-0.8, bias=-math.log(1.4))
+            nc.scalar.activation(ta[:], ya[:], ACT.Tanh, scale=0.5)
+            nc.scalar.activation(tb[:], yv[:], ACT.Tanh, bias=VEL_SHIFT)
+            nc.scalar.activation(vel[:], yv[:], ACT.Tanh)
+            nc.scalar.activation(speed[:], vel[:], ACT.Abs)
+
+            a, b, c, frc, a2, pw = [buf(n) for n in ("a", "b", "c", "frc", "a2", "pw")]
+            nc.vector.scalar_tensor_tensor(a[:], ta[:], 1.0, bell[:], ALU.add, ALU.mult)
+            nc.vector.scalar_tensor_tensor(a2[:], ta[:], 2.0, ta[:], ALU.add, ALU.mult)
+            nc.vector.scalar_tensor_tensor(b[:], tb[:], 1.0, a[:], ALU.subtract, ALU.mult)
+            nc.vector.scalar_tensor_tensor(c[:], grow[:], 0.4, b[:], ALU.max, ALU.subtract)
+            for d in range(D):
+                nc.vector.tensor_scalar(frc[:, d, :], c[:, d, :], -0.4, force[:, d : d + 1], ALU.add, ALU.mult)
+            pair = work.tile([P, 2, P], F32, name="pair")
+            nc.vector.tensor_tensor(pair[:], frc[:, 0:2, :], frc[:, 2:4, :], ALU.max)
+            peak = work.tile([P, P], F32, name="peak")
+            nc.vector.tensor_tensor(peak[:], pair[:, 0, :], pair[:, 1, :], ALU.max)
+            nc.vector.scalar_tensor_tensor(pw[:], speed[:], 1.0 / SQ_WEIGHT, frc[:], ALU.mult, ALU.mult)
+
+            total = psum.tile([P, V], F32, name="total", tag=("total" if h == 0 else "y_len0"))
+            peak_t = psum.tile([P, V], F32, name="peak_t", tag=("peak_t" if h == 0 else "y_act0"))
+            for d in range(D):
+                nc.tensor.matmul(total[:], a2[:, d, :], ident[:], start=(d == 0), stop=False, is_transpose=True)
+            nc.tensor.transpose(peak_t[:], peak[:], ident[:])
+            for d in range(D):
+                nc.tensor.matmul(total[:], pw[:, d, :], ident[:], start=False, stop=(d == D - 1), is_transpose=True)
+            weighted = work.tile([P, V], F32, name="weighted")
+            nc.scalar.activation(weighted[:], peak_t[:], ACT.Identity, scale=peak_w[:, h : h + 1], bias=-0.3)
+            result = work.tile([P, V], F32, name="result")
+            nc.vector.scalar_tensor_tensor(result[:], total[:], SQ_WEIGHT, weighted[:], ALU.mult, ALU.subtract)
+            nc.sync.dma_start(out[h * P : (h + 1) * P, :], result[:])

@@ -22,51 +22,53 @@ ACT = mybir.ActivationFunctionType
 
 VEL_SHIFT = 0.5 * math.log(1.9 / 0.7)
 SQ_WEIGHT = 0.3 / 4
+PASSIVE = 0.4
+
+BLOCK = 32
+WEIGHT_BYTES = 4 * PACK * N
+FORCE_AT = 4 * T
+PEAK_W_AT = FORCE_AT + BLOCK
+WEIGHTS_AT = PEAK_W_AT + BLOCK
+
+PAIRS = [slice(0, 2), slice(2, 4)]
 
 
 def tile_picked_yhillm_eff_p_kernel(tc, x_words, x_scales, w1, w2, w3, fmax, wl, offs, out):
     nc = tc.nc
     with ExitStack() as ctx:
         keep = ctx.enter_context(tc.tile_pool(name="keep", bufs=1))
-        work = ctx.enter_context(tc.tile_pool(name="work", bufs=2))
+        late = ctx.enter_context(tc.tile_pool(name="late", bufs=1))
         psum = ctx.enter_context(tc.psum_pool(name="psum", bufs=1))
 
         offsets = keep.tile([P, S // 16], U16, name="offsets")
         nc.sync.dma_start(offsets[:], offs)
+        raw = {"len": keep.tile([P, PACK, N], F32, name="raw_len")[:]}
+        nc.sync.dma_start(raw["len"], w1.rearrange("(p j) c -> p j c", j=PACK))
 
+        zeros = late.tile([P, PACK * N + P], F32, name="zeros", offset=FORCE_AT - BLOCK)[:, :P]
+        nc.vector.memset(zeros, 0.0)
         scale_table = keep.tile([P, T], U8, name="scale_table", align_bytes=64)
         nc.vector.memset(scale_table[:].bitcast(I32), 0)
         for q in range(4):
-            nc.scalar.dma_start(
+            (nc.sync if q % 2 == 0 else nc.scalar).dma_start(
                 scale_table[32 * q : 32 * q + 4, :].bitcast(I32),
                 x_scales[0, 4 * q : 4 * q + 4, :].bitcast(I32),
             )
-        word_table = keep.tile([P, T], I32, name="word_table", align_bytes=64)
-        nc.sync.dma_start(word_table[:], x_words[0].rearrange("p c r -> p (c r)").bitcast(I32))
 
-        zeros = keep.tile([P, P], F32, name="zeros", tag="floats")
-        nc.vector.memset(zeros[:], 0.0)
         ident = keep.tile([P, P], F32, name="ident")
-        nc.gpsimd.affine_select(out=ident[:], in_=zeros[:], compare_op=ALU.not_equal, fill=1.0, base=0,
+        nc.gpsimd.affine_select(out=ident[:], in_=zeros, compare_op=ALU.not_equal, fill=1.0, base=0,
                                 pattern=[[-1, P]], channel_multiplier=1)
 
-        floats = keep.tile([P, 3 * PACK * N + 16], F32, name="floats", tag="floats")
-        raw = {}
-        for i, (name, w) in enumerate((("len", w1), ("act", w3), ("vel", w2))):
-            raw[name] = floats[:, i * PACK * N : (i + 1) * PACK * N].rearrange("p (j c) -> p j c", j=PACK)
+        word_table = late.tile([P, T], I32, name="word_table", offset=0)
+        nc.sync.dma_start(word_table[:], x_words[0].rearrange("p c r -> p (c r)").bitcast(I32))
+        for i, (name, w) in enumerate((("act", w3), ("vel", w2))):
+            raw[name] = late.tile([P, PACK, N], F32, name="raw_" + name, offset=WEIGHTS_AT + i * WEIGHT_BYTES)[:]
             nc.sync.dma_start(raw[name], w.rearrange("(p j) c -> p j c", j=PACK))
-        force = floats[:, 3 * PACK * N : 3 * PACK * N + D]
+        force = late.tile([P, D], F32, name="force", offset=FORCE_AT)[:]
         nc.sync.dma_start(force, fmax[0, :].rearrange("(v d) -> v d", d=D))
-        peak_w = floats[:, 3 * PACK * N + 8 : 3 * PACK * N + 8 + HALVES]
+        peak_w = late.tile([P, HALVES], F32, name="peak_w", offset=PEAK_W_AT)[:]
         with nc.allow_non_contiguous_dma(reason="one weight a task row"):
             nc.sync.dma_start(peak_w, wl.rearrange("(h p) o -> p (h o)", p=P))
-
-        picked_scales = keep.tile([P, S], U8, name="picked_scales", align_bytes=64)
-        nc.vector.tensor_copy(picked_scales[:], scale_table[:].indirect(offsets[:]))
-        x_scale = keep.tile([P, D, V], U8, name="x_scale", align_bytes=64)
-        nc.vector.tensor_copy(x_scale[:], picked_scales[:].rearrange("p (v d) -> p d v", d=D))
-        x_codes = keep.tile([P, D, V], U32, name="x_codes", align_bytes=64)
-        nc.vector.tensor_copy(x_codes[:].rearrange("p d v -> p v d"), word_table[:].bitcast(U32).indirect(offsets[:]))
 
         def weave(name, h, on_scalar):
             grouped = keep.tile([P, P, PACK], BF16, name="grouped_%s%d" % (name, h), align_bytes=64)
@@ -78,60 +80,102 @@ def tile_picked_yhillm_eff_p_kernel(tc, x_words, x_scales, w1, w2, w3, fmax, wl,
                 nc.vector.tensor_copy(dst, src)
             return grouped
 
-        def product(name, h, grouped):
-            codes = keep.tile([P, P], U32, name="codes_%s%d" % (name, h), align_bytes=64)
+        def quantise(name, h, grouped, codes_tag):
+            codes = keep.tile([P, P], U32, name="codes_%s%d" % (name, h), align_bytes=64, tag=codes_tag)
             scales = keep.tile([P, P], U8, name="scales_%s%d" % (name, h), align_bytes=64)
             nc.vector.quantize_mx(out=codes[:].bitcast(FP8X4), scales=scales[:], in_=grouped[:].rearrange("p c j -> p (c j)"))
-            y = psum.tile([P, D, P], F32, name="y_%s%d" % (name, h))
-            for d in range(D):
+            return codes, scales
+
+        quantised = {}
+        woven_len = [weave("len", h, True) for h in range(HALVES)]
+        quantised["len", 0] = quantise("len", 0, woven_len[0], "codes_len0")
+
+        picked_scales = keep.tile([P, S], U8, name="picked_scales", align_bytes=64)
+        nc.vector.tensor_copy(picked_scales[:], scale_table[:].indirect(offsets[:]))
+        x_scale = keep.tile([P, D, V], U8, name="x_scale", align_bytes=64)
+        nc.vector.tensor_copy(x_scale[:], picked_scales[:].rearrange("p (v d) -> p d v", d=D))
+        x_codes = keep.tile([P, D, V], U32, name="x_codes", align_bytes=64)
+        nc.vector.tensor_copy(x_codes[:].rearrange("p d v -> p v d"), word_table[:].bitcast(U32).indirect(offsets[:]))
+
+        def product(name, h, members, tag, bufs):
+            codes, scales = quantised[name, h]
+            y = psum.tile([P, len(members), P], F32, name="y_" + name, tag=tag, bufs=bufs)
+            for i, d in enumerate(members):
                 nc.tensor.matmul_mx(
-                    out=y[:, d, :], lhsT=x_codes[:, d, :].bitcast(FP8X4), lhsT_scale=x_scale[:, d, :],
+                    out=y[:, i, :], lhsT=x_codes[:, d, :].bitcast(FP8X4), lhsT_scale=x_scale[:, d, :],
                     rhs=codes[:].bitcast(FP8X4), rhs_scale=scales[:], start=True, stop=True,
                 )
             return y
 
-        y = {}
-        for name in ("len", "act", "vel"):
-            g = [weave(name, h, name == "len") for h in range(HALVES)]
-            for h in range(HALVES):
-                y[name, h] = product(name, h, g[h])
+        for name, h in (("act", 0), ("vel", 0), ("act", 1), ("vel", 1)):
+            quantised[name, h] = quantise(name, h, weave(name, h, (name, h) == ("act", 0)), "codes_%s%d" % (name, h))
+            if (name, h) == ("vel", 0):
+                quantised["len", 1] = quantise("len", 1, woven_len[1], "grouped_vel0")
 
-        def buf(name):
-            return work.tile([P, D, P], F32, name=name)
+        def buf(name, h):
+            return keep.tile([P, D, P], F32, name="%s%d" % (name, h))
 
+        y_vel, ta, frc, peak, sq, shifted = {}, {}, {}, {}, {}, {}
         for h in range(HALVES):
-            yl, ya, yv = y["len", h], y["act", h], y["vel", h]
-            sq, bell, grow, ta, tb, vel, speed = [buf(n) for n in ("sq", "bell", "grow", "ta", "tb", "vel", "speed")]
-            nc.scalar.activation(sq[:], yl[:], ACT.Square)
-            nc.scalar.activation(grow[:], yl[:], ACT.Exp, scale=0.9, bias=math.log(0.4))
-            nc.scalar.activation(bell[:], sq[:], ACT.Exp, scale=-0.8, bias=-math.log(1.4))
-            nc.scalar.activation(ta[:], ya[:], ACT.Tanh, scale=0.5)
-            nc.scalar.activation(tb[:], yv[:], ACT.Tanh, bias=VEL_SHIFT)
-            nc.scalar.activation(vel[:], yv[:], ACT.Tanh)
-            nc.scalar.activation(speed[:], vel[:], ACT.Abs)
+            if h == 0:
+                pieces = PAIRS
+                y_len = [product("len", 0, range(2), "y_len", 2), product("len", 0, range(2, 4), "total0", 1)]
+                y_act = [product("act", 0, range(2), "y_act", 1), product("act", 0, range(2, 4), "total1", 1)]
+            else:
+                pieces = [slice(0, D)]
+                y_len, y_act = [product("len", 1, range(D), "y_len", 2)], [product("act", 1, range(D), "y_act", 1)]
+            y_vel[h] = product("vel", h, range(D), "y_vel", 2)
+            bell, tb, rise, active, shifted[h] = [buf(n, h) for n in ("bell", "tb", "rise", "active", "shifted")]
+            ta[h], frc[h] = buf("ta", h), buf("frc", h)
+            sq[h] = keep.tile([P, D, P], F32, name="sq%d" % h, tag=("grouped_act0" if h == 0 else "sq1"), align_bytes=64)[:]
+            grow = sq[h] if h == 0 else buf("grow", h)[:]
+            for i, e in enumerate(pieces):
+                nc.scalar.activation(sq[h][:, e, :], y_len[i][:], ACT.Square)
+            for i, e in enumerate(pieces):
+                nc.scalar.activation(ta[h][:, e, :], y_act[i][:], ACT.Tanh, scale=0.5)
+                nc.scalar.activation(bell[:, e, :], sq[h][:, e, :], ACT.Exp, scale=-0.8, bias=-math.log(1.4))
+            nc.scalar.activation(tb[:], y_vel[h][:], ACT.Tanh, bias=VEL_SHIFT)
+            for i, e in enumerate(pieces):
+                nc.scalar.activation(grow[:, e, :], y_len[i][:], ACT.Exp, scale=0.9, bias=math.log(PASSIVE))
 
-            a, b, c, frc, a2, pw = [buf(n) for n in ("a", "b", "c", "frc", "a2", "pw")]
-            nc.vector.scalar_tensor_tensor(a[:], ta[:], 1.0, bell[:], ALU.add, ALU.mult)
-            nc.vector.scalar_tensor_tensor(a2[:], ta[:], 2.0, ta[:], ALU.add, ALU.mult)
-            nc.vector.scalar_tensor_tensor(b[:], tb[:], 1.0, a[:], ALU.subtract, ALU.mult)
-            nc.vector.scalar_tensor_tensor(c[:], grow[:], 0.4, b[:], ALU.max, ALU.subtract)
+            for e in PAIRS:
+                nc.vector.scalar_tensor_tensor(rise[:, e, :], ta[h][:, e, :], 1.0, bell[:, e, :], ALU.add, ALU.mult)
+            for e in PAIRS:
+                nc.vector.scalar_tensor_tensor(active[:, e, :], tb[:, e, :], 1.0, rise[:, e, :], ALU.subtract, ALU.mult)
+            for e in PAIRS:
+                nc.vector.scalar_tensor_tensor(shifted[h][:, e, :], grow[:, e, :], PASSIVE, active[:, e, :], ALU.max, ALU.subtract)
             for d in range(D):
-                nc.vector.tensor_scalar(frc[:, d, :], c[:, d, :], -0.4, force[:, d : d + 1], ALU.add, ALU.mult)
-            pair = work.tile([P, 2, P], F32, name="pair")
-            nc.vector.tensor_tensor(pair[:], frc[:, 0:2, :], frc[:, 2:4, :], ALU.max)
-            peak = work.tile([P, P], F32, name="peak")
-            nc.vector.tensor_tensor(peak[:], pair[:, 0, :], pair[:, 1, :], ALU.max)
-            nc.vector.scalar_tensor_tensor(pw[:], speed[:], 1.0 / SQ_WEIGHT, frc[:], ALU.mult, ALU.mult)
+                nc.vector.tensor_scalar(frc[h][:, d, :], shifted[h][:, d, :], -PASSIVE, force[:, d : d + 1], ALU.add, ALU.mult)
+            pair_peak = keep.tile([P, 2, P], F32, name="pair_peak%d" % h)
+            for i in range(2):
+                nc.vector.tensor_tensor(pair_peak[:, i, :], frc[h][:, 2 * i, :], frc[h][:, 2 * i + 1, :], ALU.max)
+            peak[h] = keep.tile([P, P], F32, name="peak%d" % h)
+            nc.vector.tensor_tensor(peak[h][:], pair_peak[:, 0, :], pair_peak[:, 1, :], ALU.max)
 
-            total = psum.tile([P, V], F32, name="total", tag=("total" if h == 0 else "y_len0"))
-            peak_t = psum.tile([P, V], F32, name="peak_t", tag=("peak_t" if h == 0 else "y_act0"))
-            for d in range(D):
-                nc.tensor.matmul(total[:], a2[:, d, :], ident[:], start=(d == 0), stop=False, is_transpose=True)
-            nc.tensor.transpose(peak_t[:], peak[:], ident[:])
-            for d in range(D):
-                nc.tensor.matmul(total[:], pw[:, d, :], ident[:], start=False, stop=(d == D - 1), is_transpose=True)
-            weighted = work.tile([P, V], F32, name="weighted")
-            nc.scalar.activation(weighted[:], peak_t[:], ACT.Identity, scale=peak_w[:, h : h + 1], bias=-0.3)
-            result = work.tile([P, V], F32, name="result")
+        peak_t = psum.tile([P, HALVES, V], F32, name="peak_t")
+        squared = [buf("squared", h) for h in range(HALVES)]
+        nc.vector.scalar_tensor_tensor(squared[0][:], ta[0][:], 2.0, ta[0][:], ALU.add, ALU.mult)
+        nc.scalar.activation(squared[1][:], ta[1][:], ACT.Square, bias=1.0)
+        left_out = [0.3, 0.0]
+        vel = [sq[1], shifted[0][:]]
+        for h in range(HALVES):
+            nc.scalar.activation(vel[h], y_vel[h][:], ACT.Tanh)
+        sums = []
+        for h in range(HALVES):
+            speed, power = [buf(n, h) for n in ("speed", "power")]
+            nc.scalar.activation(speed[:], vel[h], ACT.Abs)
+            nc.tensor.transpose(peak_t[:, h, :], peak[h][:], ident[:])
+            weighted = keep.tile([P, V], F32, name="weighted%d" % h)
+            nc.scalar.activation(weighted[:], peak_t[:, h, :], ACT.Identity, scale=peak_w[:, h : h + 1], bias=0.0 - left_out[h])
+            for e in (PAIRS if h == 0 else [slice(0, 2), slice(2, 3), slice(3, 4)]):
+                nc.vector.scalar_tensor_tensor(power[:, e, :], speed[:, e, :], 1.0 / SQ_WEIGHT, frc[h][:, e, :], ALU.mult, ALU.mult)
+            total = psum.tile([P, V], F32, name="total%d" % h)
+            for i, term in enumerate((squared[h], power)):
+                for d in range(D):
+                    nc.tensor.matmul(total[:], term[:, d, :], ident[:], start=(i == 0 and d == 0),
+                                     stop=(i == 1 and d == D - 1), is_transpose=True)
+            sums.append((total, weighted))
+        for h, (total, weighted) in enumerate(sums):
+            result = keep.tile([P, V], F32, name="result%d" % h)
             nc.vector.scalar_tensor_tensor(result[:], total[:], SQ_WEIGHT, weighted[:], ALU.mult, ALU.subtract)
             nc.sync.dma_start(out[h * P : (h + 1) * P, :], result[:])

import math
from contextlib import ExitStack

import concourse.mybir as mybir

K, T, S, D, N = 512, 2048, 512, 4, 256
P = 128
PACK = 4
V = S // D
HALVES = N // P
FLOPS = 3 * 2 * K * N * S

F32 = mybir.dt.float32
BF16 = mybir.dt.bfloat16
I32 = mybir.dt.int32
U32 = mybir.dt.uint32
U16 = mybir.dt.uint16
U8 = mybir.dt.uint8
FP8X4 = mybir.dt.float8_e4m3fn_x4
ALU = mybir.AluOpType
ACT = mybir.ActivationFunctionType

VEL_SHIFT = 0.5 * math.log(1.9 / 0.7)
SQ_WEIGHT = 0.3 / 4
PASSIVE = 0.4

BLOCK = 32
WEIGHT_BYTES = 4 * PACK * N
FORCE_AT = 4 * T
PEAK_W_AT = FORCE_AT + BLOCK
WEIGHTS_AT = PEAK_W_AT + BLOCK

PAIRS = [slice(0, 2), slice(2, 4)]


def tile_picked_yhillm_eff_p_kernel(tc, x_words, x_scales, w1, w2, w3, fmax, wl, offs, out):
    nc = tc.nc
    with ExitStack() as ctx:
        keep = ctx.enter_context(tc.tile_pool(name="keep", bufs=1))
        late = ctx.enter_context(tc.tile_pool(name="late", bufs=1))
        psum = ctx.enter_context(tc.psum_pool(name="psum", bufs=1))

        offsets = keep.tile([P, S // 16], U16, name="offsets")
        nc.sync.dma_start(offsets[:], offs)
        raw = {"len": keep.tile([P, PACK, N], F32, name="raw_len")[:]}
        nc.sync.dma_start(raw["len"], w1.rearrange("(p j) c -> p j c", j=PACK))

        zeros = late.tile([P, PACK * N + P], F32, name="zeros", offset=FORCE_AT - BLOCK)[:, :P]
        nc.vector.memset(zeros, 0.0)
        scale_table = keep.tile([P, T], U8, name="scale_table", align_bytes=64)
        nc.vector.memset(scale_table[:].bitcast(I32), 0)
        for q in range(4):
            (nc.sync if q % 2 == 0 else nc.scalar).dma_start(
                scale_table[32 * q : 32 * q + 4, :].bitcast(I32),
                x_scales[0, 4 * q : 4 * q + 4, :].bitcast(I32),
            )

        ident = keep.tile([P, P], F32, name="ident")
        nc.gpsimd.affine_select(out=ident[:], in_=zeros, compare_op=ALU.not_equal, fill=1.0, base=0,
                                pattern=[[-1, P]], channel_multiplier=1)

        word_table = late.tile([P, T], I32, name="word_table", offset=0)
        nc.sync.dma_start(word_table[:], x_words[0].rearrange("p c r -> p (c r)").bitcast(I32))
        for i, (name, w) in enumerate((("act", w3), ("vel", w2))):
            raw[name] = late.tile([P, PACK, N], F32, name="raw_" + name, offset=WEIGHTS_AT + i * WEIGHT_BYTES)[:]
            nc.sync.dma_start(raw[name], w.rearrange("(p j) c -> p j c", j=PACK))
        force = late.tile([P, D], F32, name="force", offset=FORCE_AT)[:]
        nc.sync.dma_start(force, fmax[0, :].rearrange("(v d) -> v d", d=D))
        peak_w = late.tile([P, HALVES], F32, name="peak_w", offset=PEAK_W_AT)[:]
        with nc.allow_non_contiguous_dma(reason="one weight a task row"):
            nc.sync.dma_start(peak_w, wl.rearrange("(h p) o -> p (h o)", p=P))

        def weave(name, h, on_scalar):
            grouped = keep.tile([P, P, PACK], BF16, name="grouped_%s%d" % (name, h), align_bytes=64)
            dst = grouped[:].rearrange("p (c i) j -> p c j i", i=4)
            src = raw[name][:, :, h * P : (h + 1) * P].rearrange("p j (c i) -> p c j i", i=4)
            if on_scalar:
                nc.scalar.activation(dst, src, ACT.Copy)
            else:
                nc.vector.tensor_copy(dst, src)
            return grouped

        def quantise(name, h, grouped, codes_tag):
            codes = keep.tile([P, P], U32, name="codes_%s%d" % (name, h), align_bytes=64, tag=codes_tag)
            scales = keep.tile([P, P], U8, name="scales_%s%d" % (name, h), align_bytes=64)
            nc.vector.quantize_mx(out=codes[:].bitcast(FP8X4), scales=scales[:], in_=grouped[:].rearrange("p c j -> p (c j)"))
            return codes, scales

        quantised = {}
        woven_len = [weave("len", h, True) for h in range(HALVES)]
        quantised["len", 0] = quantise("len", 0, woven_len[0], "codes_len0")

        picked_scales = keep.tile([P, S], U8, name="picked_scales", align_bytes=64)
        nc.vector.tensor_copy(picked_scales[:], scale_table[:].indirect(offsets[:]))
        x_scale = keep.tile([P, D, V], U8, name="x_scale", align_bytes=64)
        nc.vector.tensor_copy(x_scale[:], picked_scales[:].rearrange("p (v d) -> p d v", d=D))
        x_codes = keep.tile([P, D, V], U32, name="x_codes", align_bytes=64)
        nc.vector.tensor_copy(x_codes[:].rearrange("p d v -> p v d"), word_table[:].bitcast(U32).indirect(offsets[:]))

        def product(name, h, members, tag, bufs):
            codes, scales = quantised[name, h]
            y = psum.tile([P, len(members), P], F32, name="y_" + name, tag=tag, bufs=bufs)
            for i, d in enumerate(members):
                nc.tensor.matmul_mx(
                    out=y[:, i, :], lhsT=x_codes[:, d, :].bitcast(FP8X4), lhsT_scale=x_scale[:, d, :],
                    rhs=codes[:].bitcast(FP8X4), rhs_scale=scales[:], start=True, stop=True,
                )
            return y

        for name, h in (("act", 0), ("vel", 0), ("act", 1), ("vel", 1)):
            quantised[name, h] = quantise(name, h, weave(name, h, (name, h) == ("act", 0)), "codes_%s%d" % (name, h))
            if (name, h) == ("vel", 0):
                quantised["len", 1] = quantise("len", 1, woven_len[1], "grouped_vel0")

        def buf(name, h):
            return keep.tile([P, D, P], F32, name="%s%d" % (name, h))

        y_vel, ta, frc, peak, sq, shifted = {}, {}, {}, {}, {}, {}
        for h in range(HALVES):
            if h == 0:
                pieces = PAIRS
                y_len = [product("len", 0, range(2), "y_len", 2), product("len", 0, range(2, 4), "total0", 1)]
                y_act = [product("act", 0, range(2), "y_act", 1), product("act", 0, range(2, 4), "total1", 1)]
            else:
                pieces = [slice(0, D)]
                y_len, y_act = [product("len", 1, range(D), "y_len", 2)], [product("act", 1, range(D), "y_act", 1)]
            y_vel[h] = product("vel", h, range(D), "y_vel", 2)
            bell, tb, rise, active, shifted[h] = [buf(n, h) for n in ("bell", "tb", "rise", "active", "shifted")]
            ta[h], frc[h] = buf("ta", h), buf("frc", h)
            sq[h] = keep.tile([P, D, P], F32, name="sq%d" % h, tag=("grouped_act0" if h == 0 else "sq1"), align_bytes=64)[:]
            grow = sq[h] if h == 0 else buf("grow", h)[:]
            for i, e in enumerate(pieces):
                nc.scalar.activation(sq[h][:, e, :], y_len[i][:], ACT.Square)
            for i, e in enumerate(pieces):
                nc.scalar.activation(ta[h][:, e, :], y_act[i][:], ACT.Tanh, scale=0.5)
                nc.scalar.activation(bell[:, e, :], sq[h][:, e, :], ACT.Exp, scale=-0.8, bias=-math.log(1.4))
            nc.scalar.activation(tb[:], y_vel[h][:], ACT.Tanh, bias=VEL_SHIFT)
            for i, e in enumerate(pieces):
                nc.scalar.activation(grow[:, e, :], y_len[i][:], ACT.Exp, scale=0.9, bias=math.log(PASSIVE))

            for e in PAIRS:
                nc.vector.scalar_tensor_tensor(rise[:, e, :], ta[h][:, e, :], 1.0, bell[:, e, :], ALU.add, ALU.mult)
            for e in PAIRS:
                nc.vector.scalar_tensor_tensor(active[:, e, :], tb[:, e, :], 1.0, rise[:, e, :], ALU.subtract, ALU.mult)
            for e in PAIRS:
                nc.vector.scalar_tensor_tensor(shifted[h][:, e, :], grow[:, e, :], PASSIVE, active[:, e, :], ALU.max, ALU.subtract)
            for d in range(D):
                nc.vector.tensor_scalar(frc[h][:, d, :], shifted[h][:, d, :], -PASSIVE, force[:, d : d + 1], ALU.add, ALU.mult)
            pair_peak = keep.tile([P, 2, P], F32, name="pair_peak%d" % h)
            for i in range(2):
                nc.vector.tensor_tensor(pair_peak[:, i, :], frc[h][:, 2 * i, :], frc[h][:, 2 * i + 1, :], ALU.max)
            peak[h] = keep.tile([P, P], F32, name="peak%d" % h)
            nc.vector.tensor_tensor(peak[h][:], pair_peak[:, 0, :], pair_peak[:, 1, :], ALU.max)

        peak_t = psum.tile([P, HALVES, V], F32, name="peak_t")
        squared = [buf("squared", h) for h in range(HALVES)]
        nc.vector.scalar_tensor_tensor(squared[0][:], ta[0][:], 2.0, ta[0][:], ALU.add, ALU.mult)
        nc.scalar.activation(squared[1][:], ta[1][:], ACT.Square, bias=1.0)
        left_out = [0.3, 0.0]
        vel = [sq[1], shifted[0][:]]
        for h in range(HALVES):
            nc.scalar.activation(vel[h], y_vel[h][:], ACT.Tanh)
        sums = []
        for h in range(HALVES):
            speed, power = [buf(n, h) for n in ("speed", "power")]
            nc.scalar.activation(speed[:], vel[h], ACT.Abs)
            nc.tensor.transpose(peak_t[:, h, :], peak[h][:], ident[:])
            weighted = keep.tile([P, V], F32, name="weighted%d" % h)
            nc.scalar.activation(weighted[:], peak_t[:, h, :], ACT.Identity, scale=peak_w[:, h : h + 1], bias=0.0 - left_out[h])
            for e in (PAIRS if h == 0 else [slice(0, 2), slice(2, 3), slice(3, 4)]):
                nc.vector.scalar_tensor_tensor(power[:, e, :], speed[:, e, :], 1.0 / SQ_WEIGHT, frc[h][:, e, :], ALU.mult, ALU.mult)
            total = psum.tile([P, V], F32, name="total%d" % h)
            for i, term in enumerate((squared[h], power)):
                for d in range(D):
                    nc.tensor.matmul(total[:], term[:, d, :], ident[:], start=(i == 0 and d == 0),
                                     stop=(i == 1 and d == D - 1), is_transpose=True)
            sums.append((total, weighted))
        for h, (total, weighted) in enumerate(sums):
            result = keep.tile([P, V], F32, name="result%d" % h)
            nc.vector.scalar_tensor_tensor(result[:], total[:], SQ_WEIGHT, weighted[:], ALU.mult, ALU.subtract)
            nc.sync.dma_start(out[h * P : (h + 1) * P, :], result[:])
